import numpy as np
import ml_dtypes


def mxq(x, axis, fmt="e4m3"):
    dtype, down = {"e4m3": (ml_dtypes.float8_e4m3fn, 7), "e5m2": (ml_dtypes.float8_e5m2, 14)}[fmt]
    v = np.moveaxis(np.asarray(x, np.float32).astype(ml_dtypes.bfloat16).astype(np.float64), axis, -1)
    blocks = v.reshape(v.shape[:-1] + (-1, 32))
    amax = np.abs(blocks).max(-1, keepdims=True)
    byte = np.maximum(np.where(amax > 0, np.frexp(amax)[1] - 1 + 127, 0) - down, 1)
    scale = np.exp2(byte - 127.0)
    codes = (blocks / scale).astype(np.float32).astype(dtype).astype(np.float64)
    return np.moveaxis((codes * scale).reshape(v.shape), -1, axis)


WIDE = False


def mx_kscale(k):
    if not WIDE:
        return np.ones(k)
    levels = np.array([10, -10, 5, -5, 0])
    if k % 512:
        return np.exp2(np.random.permutation(np.resize(levels, k // 32))).repeat(32)
    a = np.empty((k // 512, 16))
    for p in range(k // 512):
        a[p, :8] = np.random.permutation(np.resize(levels, 8))
        for g in range(8):
            far = levels[np.abs(levels - a[p, g]) >= 10]
            a[p, g + 8] = far[np.random.randint(len(far))]
    return np.exp2(a.ravel()).repeat(32)


def f64(x):
    return np.asarray(x).astype(np.float64)


def striped(idx):
    return np.tile(idx.reshape(-1, 16).T, (8, 1)).astype(np.uint16)


def unstriped(offs):
    return offs[:16].T.reshape(-1).astype(np.int64)


def striped8(idx):
    return np.concatenate([x.reshape(-1, 16).T for x in idx]).astype(np.uint16)


def runs(offs, k):
    lists = np.stack([offs[16 * r : 16 * r + 16].T.reshape(-1) for r in range(8)]).astype(np.int64)
    return lists[np.arange(k) % 512 // 64]


def pack_weight(w):
    k, n = w.shape
    w = f64(np.asarray(w, np.float32).astype(ml_dtypes.bfloat16)).reshape(k // 32, 32, n)
    amax = np.abs(w).max(1)
    byte = np.clip(np.where(amax > 0, np.frexp(amax)[1] - 1 + 127 - 7, 1), 1, 254)
    scaled = (w * np.exp2(127.0 - byte)[:, None, :]).reshape(k, n).astype(np.float32)
    words = np.ascontiguousarray(scaled.reshape(k // 512, 128, 4, n).transpose(0, 1, 3, 2)).astype(ml_dtypes.float8_e4m3fn).view(np.uint8)
    return words, np.ascontiguousarray(byte.astype(np.uint8).reshape(k // 512, 16, n))


def unpack_weight(words, scales):
    g, p, n, _ = words.shape
    vals = np.ascontiguousarray(words).view(ml_dtypes.float8_e4m3fn).astype(np.float64) * np.repeat(np.exp2(scales.astype(np.float64) - 127.0), 8, axis=1)[..., None]
    return vals.transpose(0, 1, 3, 2).reshape(g * 512, n)

def planes(y):
    n, m = y.shape
    v = y.astype(np.float32).astype(ml_dtypes.bfloat16).astype(np.float64).reshape(n // 32, 32, m)
    top = np.abs(v).max(1)
    byte = np.clip(np.where(top > 0, np.frexp(top)[1] - 1 + 127 - 7, 1), 1, 254)
    codes = (v * np.exp2(127.0 - byte)[:, None, :]).reshape(n, m).astype(np.float32).astype(ml_dtypes.float8_e4m3fn).view(np.uint8)
    words = codes.reshape(n // 512, 128, 4, m).transpose(0, 1, 3, 2)
    return np.ascontiguousarray(words), np.ascontiguousarray(byte.astype(np.uint8).reshape(n // 512, 16, m))


K, T, S, V, N, H = 512, 2048, 512, 256, 512, 512


def setup_inputs():
    n = np.random.standard_normal
    s = mx_kscale(K)[:, None]
    u = mx_kscale(S)
    packed_xT = pack_weight(n((K, T)) * s)
    perm = np.stack([np.random.permutation(H) for _ in range(8)])
    return {
        "x_words": packed_xT[0],
        "x_scales": packed_xT[1],
        "wa": (n((K, H)) / np.sqrt(K) / s).astype(np.float32),
        "wb": (n((K, N)) / np.sqrt(K) / s).astype(np.float32),
        "gt": (np.random.uniform(0.5, 1.5, (S, 1)) * u[:, None]).astype(np.float32),
        "gi": (np.random.uniform(0.5, 1.5, (S, 1)) / u[:, None]).astype(np.float32),
        "offs": striped(np.random.permutation(T)[:S]),
        "two": striped(np.random.permutation(T)[:S]),
        "la": striped8(perm[:, :V]),
        "lb": striped8(perm[:, V:]),
    }


def reference(x_words, x_scales, wa, wb, gt, gi, offs, two, la, lb):
    xq = unpack_weight(x_words, x_scales)[:, unstriped(offs)]
    a = xq.T @ mxq(f64(wa), 0, "e4m3")
    p = a[np.arange(S)[:, None], runs(la, S)]
    qv = a[np.arange(S)[:, None], runs(lb, S)]
    lo = np.minimum(p, qv)
    hi = np.maximum(p, qv)
    d1 = np.zeros((S, H))
    d1[np.arange(S)[:, None], runs(la, S)] = hi
    d2 = d1.copy()
    d2[np.arange(S)[:, None], runs(lb, S)] = lo
    z = f64(gt) * d2
    x_two = unpack_weight(x_words, x_scales)[:, unstriped(two)]
    b = x_two.T @ mxq(f64(wb), 0, "e4m3")
    z2 = f64(gi) * b
    cv = 0.0625 * ((mxq(z, 0, "e4m3").T @ mxq(z2, 0, "e4m3")))
    out_0 = cv
    return (out_0,) + planes(out_0)

@@ -1,0 +1,208 @@
+from contextlib import ExitStack
+
+import concourse.mybir as mybir
+
+K, T, S, V, N, H = 512, 2048, 512, 256, 512, 512
+FLOPS = 2 * K * S * H + 2 * K * S * N + 2 * S * H * N
+
+F32 = mybir.dt.float32
+BF16 = mybir.dt.bfloat16
+I32 = mybir.dt.int32
+U32 = mybir.dt.uint32
+U16 = mybir.dt.uint16
+U8 = mybir.dt.uint8
+FP8X4 = mybir.dt.float8_e4m3fn_x4
+ALU = mybir.AluOpType
+COPY = mybir.ActivationFunctionType.Copy
+
+P = 128
+PACK = 4
+RUN = 8
+HALF = H // 2
+QUARTER = N // 4
+GATE_PITCH = 8
+OUT_SCALE = 0.0625
+TILE_PAIRS = ((2, 0), (1, 3))
+
+
+def tile_picked_momord_none_po_kernel(
+    tc, x_words, x_scales, wa, wb, gt, gi, offs, two, la, lb, out_0, out_1, out_2
+):
+    nc = tc.nc
+    with ExitStack() as ctx:
+        lists = ctx.enter_context(tc.tile_pool(name="lists", bufs=1))
+        keep = ctx.enter_context(tc.tile_pool(name="keep", bufs=1))
+        psum = ctx.enter_context(tc.psum_pool(name="psum", bufs=1))
+
+        def sb(shape, dtype, name, tag=None):
+            return keep.tile(shape, dtype, name=name, tag=tag or name, align_bytes=64)
+
+        def load_list(src, name):
+            tile = lists.tile(list(src.shape), U16, name=name)
+            nc.sync.dma_start(tile[:], src)
+            return tile
+
+        def interleave_rows(dst, src):
+            nc.scalar.copy(
+                out=dst.rearrange("p (c i) j -> p c j i", i=PACK),
+                in_=src.rearrange("p j (c i) -> p c j i", i=PACK),
+            )
+
+        def quantize(codes, scales, grouped):
+            nc.vector.quantize_mx(out=codes.bitcast(FP8X4), scales=scales, in_=grouped)
+
+        def product(out, left_codes, left_scales, right_codes, right_scales):
+            nc.tensor.matmul_mx(
+                out=out,
+                lhsT=left_codes.bitcast(FP8X4),
+                lhsT_scale=left_scales,
+                rhs=right_codes.bitcast(FP8X4),
+                rhs_scale=right_scales,
+                start=True,
+                stop=True,
+            )
+
+        table_scales = sb([P, T], U8, "table_scales")
+        nc.vector.memset(table_scales[:].bitcast(I32), 0)
+        offs_sb = load_list(offs, "offs_sb")
+        two_sb = load_list(two, "two_sb")
+        la_sb = load_list(la, "la_sb")
+        lb_sb = load_list(lb, "lb_sb")
+        for quad in range(4):
+            nc.scalar.dma_start(
+                table_scales[32 * quad : 32 * quad + 4, :].bitcast(I32),
+                x_scales[0, 4 * quad : 4 * quad + 4, :].bitcast(I32),
+            )
+        table_words = sb([P, T], U32, "table_words")
+        nc.sync.dma_start(
+            table_words[:].bitcast(I32), x_words[0].rearrange("p c r -> p (c r)").bitcast(I32)
+        )
+        wa_rows = wa.rearrange("(p j) c -> p j c", j=PACK)
+        wa_raw = []
+        for half in range(2):
+            raw = sb([P, PACK, HALF], F32, f"wa_raw{half}", tag=f"raw{half}")
+            nc.sync.dma_start(raw[:], wa_rows[:, :, half * HALF : (half + 1) * HALF])
+            wa_raw.append(raw)
+        wb_raw = sb([P, PACK, N], F32, "wb_raw")
+        nc.sync.dma_start(wb_raw[:], wb.rearrange("(p j) c -> p j c", j=PACK))
+
+        def gather_words(offsets, name, tag=None):
+            words = sb([P, S], U32, name, tag)
+            nc.vector.tensor_copy(
+                out=words[:].rearrange("p (t q e) -> p q t e", t=PACK, e=RUN),
+                in_=table_words[:].indirect(offsets[:]),
+            )
+            return words
+
+        def gather_scales(offsets, name, tag=None):
+            listed = sb([P, S], U8, name + "_listed", tag)
+            nc.vector.tensor_copy(out=listed[:], in_=table_scales[:].indirect(offsets[:]))
+            dealt = sb([P, S], U8, name)
+            nc.vector.tensor_copy(
+                out=dealt[:].bitcast(I32).rearrange("p (t q e) -> p t q e", t=PACK, e=RUN // 4),
+                in_=listed[:].bitcast(I32).rearrange("p (q t e) -> p t q e", t=PACK, e=RUN // 4),
+            )
+            return dealt
+
+        xa_scales = gather_scales(offs_sb, "xa_scales", tag="small")
+        xa_words = gather_words(offs_sb, "xa_words")
+        gates = sb([P, 2, PACK, GATE_PITCH], F32, "gates", tag="small")
+        with nc.allow_non_contiguous_dma(reason="one weight for each partition"):
+            for which, src in enumerate((gt, gi)):
+                by_tile = src.rearrange("(q t e) o -> t q e o", t=PACK, e=RUN)
+                for t in range(PACK):
+                    nc.sync.dma_start(gates[:, which, t, 0:1], by_tile[t])
+        order = [t for pair in TILE_PAIRS for t in pair]
+        a_banks = {t: psum.tile([P, H], F32, name=f"a_bank{t}", tag=f"bank{t}") for t in order}
+        wa_codes = sb([P, H], U32, "wa_codes")
+        wa_scales = sb([P, H], U8, "wa_scales")
+        for half in range(2):
+            cols = slice(half * HALF, (half + 1) * HALF)
+            grouped = sb([P, HALF, PACK], BF16, f"wa_grouped{half}", tag=f"grouped{half}")
+            interleave_rows(grouped[:], wa_raw[half][:])
+            quantize(wa_codes[:, cols], wa_scales[:, cols], grouped[:].rearrange("p c j -> p (c j)"))
+            for t in order:
+                tok = slice(t * P, (t + 1) * P)
+                product(a_banks[t][:, cols], xa_words[:, tok], xa_scales[:, tok], wa_codes[:, cols], wa_scales[:, cols])
+        a_sb = {}
+        for t in order:
+            a_sb[t] = sb([P, H], F32, f"a_sb{t}")
+            nc.scalar.copy(out=a_sb[t][:], in_=a_banks[t][:])
+
+        xb_words = gather_words(two_sb, "xb_words", tag="grouped0")
+        xb_scales = gather_scales(two_sb, "xb_scales", tag="grouped1")
+
+        wb_codes = sb([P, N], U32, "wb_codes")
+        wb_scales = sb([P, N], U8, "wb_scales")
+        for half in range(2):
+            cols = slice(half * HALF, (half + 1) * HALF)
+            grouped = sb([P, HALF, PACK], BF16, f"wb_grouped{half}", tag=("xa_words", "xa_scales")[half])
+            interleave_rows(grouped[:], wb_raw[:, :, cols])
+            quantize(wb_codes[:, cols], wb_scales[:, cols], grouped[:].rearrange("p c j -> p (c j)"))
+        z2_rows = sb([P, PACK, N], BF16, "z2_rows", tag="planes")
+        for t in range(PACK):
+            tok = slice(t * P, (t + 1) * P)
+            b_bank = psum.tile([P, N], F32, name=f"b_bank{t}", tag=f"bank{PACK + t}")
+            product(b_bank[:], xb_words[:, tok], xb_scales[:, tok], wb_codes[:], wb_scales[:])
+            nc.scalar.activation(out=z2_rows[:, t, :], in_=b_bank[:], func=COPY, scale=gates[:, 1, t, 0:1])
+        z2_grouped = sb([P, N, PACK], BF16, "z2_grouped", tag="after_z2")
+        interleave_rows(z2_grouped[:], z2_rows[:])
+        z2_codes = sb([P, N], U32, "z2_codes")
+        z2_scales = sb([P, N], U8, "z2_scales")
+        quantize(z2_codes[:], z2_scales[:], z2_grouped[:].rearrange("p c j -> p (c j)"))
+
+        z_grouped = sb([P, PACK, P, PACK], BF16, "z_grouped", tag="planes")
+        window_tags = dict(zip(order, ("wb_raw", "xa_scales", "after_z2", "xa_scales")))
+        picked_tags = {order[-1]: "xa_words"}
+        for pair in TILE_PAIRS:
+            ordered = {}
+            for t in pair:
+                picked = sb([P, 2, V], F32, f"picked{t}", tag=picked_tags.get(t))
+                nc.vector.tensor_copy(out=picked[:, 0, :], in_=a_sb[t][:].indirect(la_sb[:]))
+                nc.vector.tensor_copy(out=picked[:, 1, :], in_=a_sb[t][:].indirect(lb_sb[:]))
+                ordered[t] = sb([P, 2, V], F32, f"ordered{t}")
+                nc.vector.tensor_tensor(out=ordered[t][:, 0, :], in0=picked[:, 0, :], in1=picked[:, 1, :], op=ALU.max)
+                nc.vector.tensor_tensor(out=ordered[t][:, 1, :], in0=picked[:, 0, :], in1=picked[:, 1, :], op=ALU.min)
+            windows = {t: sb([P, H], F32, f"d{t}", tag=window_tags[t]) for t in pair}
+            for t in pair:
+                nc.vector.tensor_copy(out=windows[t][:].indirect(la_sb[:]), in_=ordered[t][:, 0, :])
+            for t in pair:
+                nc.vector.tensor_copy(out=windows[t][:].indirect(lb_sb[:]), in_=ordered[t][:, 1, :])
+                plane = z_grouped[:, :, :, t].rearrange("p u m -> p m u")
+                values = windows[t][:].rearrange("p (m u) -> p m u", u=PACK)
+                if t == order[-1]:
+                    nc.vector.tensor_scalar(out=plane, in0=values, scalar1=gates[:, 0, t, 0:1], scalar2=None, op0=ALU.mult)
+                else:
+                    nc.scalar.activation(out=plane, in_=values, func=COPY, scale=gates[:, 0, t, 0:1])
+
+        z_codes = sb([P, H], U32, "z_codes")
+        z_scales = sb([P, H], U8, "z_scales")
+        for u in range(PACK):
+            rows = slice(u * P, (u + 1) * P)
+            quantize(z_codes[:, rows], z_scales[:, rows], z_grouped[:, u, :, :].rearrange("p m j -> p (m j)"))
+        out_rows = out_0.rearrange("(p u) n -> p u n", u=PACK)
+        out_words = out_1[0].rearrange("p c r -> p (c r)").bitcast(I32)
+        y_codes = sb([P, N], U32, "y_codes")
+        y_scales = sb([P, N], U8, "y_scales")
+        for c in range(N // QUARTER):
+            cols = slice(c * QUARTER, (c + 1) * QUARTER)
+            bank = psum.tile([P, PACK, QUARTER], F32, name=f"y_bank{c}", tag=f"bank{c}")
+            for u in range(PACK):
+                rows = slice(u * P, (u + 1) * P)
+                product(bank[:, u, :], z_codes[:, rows], z_scales[:, rows], z2_codes[:, cols], z2_scales[:, cols])
+            y = sb([P, PACK, QUARTER], F32, f"y{c}")
+            nc.scalar.activation(out=y[:], in_=bank[:], func=COPY, scale=OUT_SCALE)
+            nc.sync.dma_start(out_rows[:, :, cols], y[:])
+            y_grouped = sb([P, QUARTER, PACK], BF16, f"y_grouped{c}")
+            nc.vector.tensor_copy(
+                out=y_grouped[:].rearrange("p (c i) u -> p c u i", i=PACK),
+                in_=y[:].rearrange("p u (c i) -> p c u i", i=PACK),
+            )
+            quantize(y_codes[:, cols], y_scales[:, cols], y_grouped[:].rearrange("p c u -> p (c u)"))
+            nc.sync.dma_start(out_words[:, cols], y_codes[:, cols].bitcast(I32))
+        for quad in range(4):
+            queue = nc.scalar if quad % 2 else nc.sync
+            queue.dma_start(
+                out_2[0, 4 * quad : 4 * quad + 4, :].bitcast(I32),
+                y_scales[32 * quad : 32 * quad + 4, :].bitcast(I32),
+            )

@@ -22,7 +22,8 @@ HALF = H // 2
 QUARTER = N // 4
 GATE_PITCH = 8
 OUT_SCALE = 0.0625
-TILE_PAIRS = ((2, 0), (1, 3))
+ORDER = (2, 0, 1, 3)
+VECTOR_SHARE = 84
 
 
 def tile_picked_momord_none_po_kernel(
@@ -66,23 +67,21 @@ def tile_picked_momord_none_po_kernel(
         nc.vector.memset(table_scales[:].bitcast(I32), 0)
         offs_sb = load_list(offs, "offs_sb")
         two_sb = load_list(two, "two_sb")
-        la_sb = load_list(la, "la_sb")
-        lb_sb = load_list(lb, "lb_sb")
+        wa_rows = wa.rearrange("(p j) c -> p j c", j=PACK)
+        wa_raw = [sb([P, PACK, HALF], F32, f"wa_raw{half}") for half in range(2)]
+        nc.sync.dma_start(wa_raw[0][:], wa_rows[:, :, :HALF])
         for quad in range(4):
-            nc.scalar.dma_start(
+            nc.sync.dma_start(
                 table_scales[32 * quad : 32 * quad + 4, :].bitcast(I32),
                 x_scales[0, 4 * quad : 4 * quad + 4, :].bitcast(I32),
             )
+        nc.sync.dma_start(wa_raw[1][:], wa_rows[:, :, HALF:])
         table_words = sb([P, T], U32, "table_words")
         nc.sync.dma_start(
             table_words[:].bitcast(I32), x_words[0].rearrange("p c r -> p (c r)").bitcast(I32)
         )
-        wa_rows = wa.rearrange("(p j) c -> p j c", j=PACK)
-        wa_raw = []
-        for half in range(2):
-            raw = sb([P, PACK, HALF], F32, f"wa_raw{half}", tag=f"raw{half}")
-            nc.sync.dma_start(raw[:], wa_rows[:, :, half * HALF : (half + 1) * HALF])
-            wa_raw.append(raw)
+        la_sb = load_list(la, "la_sb")
+        lb_sb = load_list(lb, "lb_sb")
         wb_raw = sb([P, PACK, N], F32, "wb_raw")
         nc.sync.dma_start(wb_raw[:], wb.rearrange("(p j) c -> p j c", j=PACK))
 
@@ -104,16 +103,9 @@ def tile_picked_momord_none_po_kernel(
             )
             return dealt
 
+        order = ORDER
         xa_scales = gather_scales(offs_sb, "xa_scales", tag="small")
-        xa_words = gather_words(offs_sb, "xa_words")
-        gates = sb([P, 2, PACK, GATE_PITCH], F32, "gates", tag="small")
-        with nc.allow_non_contiguous_dma(reason="one weight for each partition"):
-            for which, src in enumerate((gt, gi)):
-                by_tile = src.rearrange("(q t e) o -> t q e o", t=PACK, e=RUN)
-                for t in range(PACK):
-                    nc.sync.dma_start(gates[:, which, t, 0:1], by_tile[t])
-        order = [t for pair in TILE_PAIRS for t in pair]
-        a_banks = {t: psum.tile([P, H], F32, name=f"a_bank{t}", tag=f"bank{t}") for t in order}
+        xb_scales = gather_scales(two_sb, "xb_scales")
         wa_codes = sb([P, H], U32, "wa_codes")
         wa_scales = sb([P, H], U8, "wa_scales")
         for half in range(2):
@@ -121,59 +113,82 @@ def tile_picked_momord_none_po_kernel(
             grouped = sb([P, HALF, PACK], BF16, f"wa_grouped{half}", tag=f"grouped{half}")
             interleave_rows(grouped[:], wa_raw[half][:])
             quantize(wa_codes[:, cols], wa_scales[:, cols], grouped[:].rearrange("p c j -> p (c j)"))
-            for t in order:
-                tok = slice(t * P, (t + 1) * P)
-                product(a_banks[t][:, cols], xa_words[:, tok], xa_scales[:, tok], wa_codes[:, cols], wa_scales[:, cols])
+        xa_words = gather_words(offs_sb, "xa_words")
+        xb_words = gather_words(two_sb, "xb_words")
         a_sb = {}
         for t in order:
+            tok = slice(t * P, (t + 1) * P)
             a_sb[t] = sb([P, H], F32, f"a_sb{t}")
-            nc.scalar.copy(out=a_sb[t][:], in_=a_banks[t][:])
+            pieces = 2 if t == order[0] else 1
+            width = H // pieces
+            for piece in range(pieces):
+                cols = slice(piece * width, (piece + 1) * width)
+                a_bank = psum.tile([P, width], F32, name=f"a_bank{t}_{piece}", tag=f"bank{PACK * piece + t}")
+                product(a_bank[:], xa_words[:, tok], xa_scales[:, tok], wa_codes[:, cols], wa_scales[:, cols])
+                nc.scalar.copy(out=a_sb[t][:, cols], in_=a_bank[:])
 
-        xb_words = gather_words(two_sb, "xb_words", tag="grouped0")
-        xb_scales = gather_scales(two_sb, "xb_scales", tag="grouped1")
+        gates = sb([P, 2 * PACK - 1, GATE_PITCH], F32, "gates", tag="grouped0")
+        first_gate = sb([P, 1], F32, "first_gate", tag="small")
+        columns = [gates[:, c, 0:1] for c in range(2 * PACK - 1)]
+        gi_cols = columns[:PACK]
+        gt_cols = dict(zip(order, [first_gate[:]] + columns[PACK:]))
+        with nc.allow_non_contiguous_dma(reason="one weight for each partition"):
+            for src, cols in ((gi, gi_cols), (gt, gt_cols)):
+                by_tile = src.rearrange("(q t e) o -> t q e o", t=PACK, e=RUN)
+                for t in range(PACK):
+                    nc.sync.dma_start(cols[t], by_tile[t])
 
+        wb_grouped = sb([P, N, PACK], BF16, "wb_grouped", tag="xa_words")
+        interleave_rows(wb_grouped[:], wb_raw[:])
         wb_codes = sb([P, N], U32, "wb_codes")
         wb_scales = sb([P, N], U8, "wb_scales")
-        for half in range(2):
-            cols = slice(half * HALF, (half + 1) * HALF)
-            grouped = sb([P, HALF, PACK], BF16, f"wb_grouped{half}", tag=("xa_words", "xa_scales")[half])
-            interleave_rows(grouped[:], wb_raw[:, :, cols])
-            quantize(wb_codes[:, cols], wb_scales[:, cols], grouped[:].rearrange("p c j -> p (c j)"))
+        quantize(wb_codes[:], wb_scales[:], wb_grouped[:].rearrange("p c j -> p (c j)"))
         z2_rows = sb([P, PACK, N], BF16, "z2_rows", tag="planes")
         for t in range(PACK):
             tok = slice(t * P, (t + 1) * P)
             b_bank = psum.tile([P, N], F32, name=f"b_bank{t}", tag=f"bank{PACK + t}")
             product(b_bank[:], xb_words[:, tok], xb_scales[:, tok], wb_codes[:], wb_scales[:])
-            nc.scalar.activation(out=z2_rows[:, t, :], in_=b_bank[:], func=COPY, scale=gates[:, 1, t, 0:1])
-        z2_grouped = sb([P, N, PACK], BF16, "z2_grouped", tag="after_z2")
+            nc.scalar.activation(out=z2_rows[:, t, :], in_=b_bank[:], func=COPY, scale=gi_cols[t])
+        z2_grouped = sb([P, N, PACK], BF16, "z2_grouped")
         interleave_rows(z2_grouped[:], z2_rows[:])
-        z2_codes = sb([P, N], U32, "z2_codes")
-        z2_scales = sb([P, N], U8, "z2_scales")
-        quantize(z2_codes[:], z2_scales[:], z2_grouped[:].rearrange("p c j -> p (c j)"))
+
+        picked = sb([P, 2, PACK, V], F32, "picked")
+        for t in order:
+            nc.vector.tensor_copy(out=picked[:, 0, t, :], in_=a_sb[t][:].indirect(la_sb[:]))
+            nc.vector.tensor_copy(out=picked[:, 1, t, :], in_=a_sb[t][:].indirect(lb_sb[:]))
+        ordered = sb([P, 2, PACK, V], F32, "ordered", tag="wb_raw")
+        nc.vector.tensor_tensor(out=ordered[:, 0], in0=picked[:, 0], in1=picked[:, 1], op=ALU.max)
+        nc.vector.tensor_tensor(out=ordered[:, 1], in0=picked[:, 0], in1=picked[:, 1], op=ALU.min)
 
         z_grouped = sb([P, PACK, P, PACK], BF16, "z_grouped", tag="planes")
-        window_tags = dict(zip(order, ("wb_raw", "xa_scales", "after_z2", "xa_scales")))
-        picked_tags = {order[-1]: "xa_words"}
-        for pair in TILE_PAIRS:
-            ordered = {}
-            for t in pair:
-                picked = sb([P, 2, V], F32, f"picked{t}", tag=picked_tags.get(t))
-                nc.vector.tensor_copy(out=picked[:, 0, :], in_=a_sb[t][:].indirect(la_sb[:]))
-                nc.vector.tensor_copy(out=picked[:, 1, :], in_=a_sb[t][:].indirect(lb_sb[:]))
-                ordered[t] = sb([P, 2, V], F32, f"ordered{t}")
-                nc.vector.tensor_tensor(out=ordered[t][:, 0, :], in0=picked[:, 0, :], in1=picked[:, 1, :], op=ALU.max)
-                nc.vector.tensor_tensor(out=ordered[t][:, 1, :], in0=picked[:, 0, :], in1=picked[:, 1, :], op=ALU.min)
-            windows = {t: sb([P, H], F32, f"d{t}", tag=window_tags[t]) for t in pair}
-            for t in pair:
-                nc.vector.tensor_copy(out=windows[t][:].indirect(la_sb[:]), in_=ordered[t][:, 0, :])
-            for t in pair:
-                nc.vector.tensor_copy(out=windows[t][:].indirect(lb_sb[:]), in_=ordered[t][:, 1, :])
-                plane = z_grouped[:, :, :, t].rearrange("p u m -> p m u")
-                values = windows[t][:].rearrange("p (m u) -> p m u", u=PACK)
-                if t == order[-1]:
-                    nc.vector.tensor_scalar(out=plane, in0=values, scalar1=gates[:, 0, t, 0:1], scalar2=None, op0=ALU.mult)
-                else:
-                    nc.scalar.activation(out=plane, in_=values, func=COPY, scale=gates[:, 0, t, 0:1])
+
+        def plane(t, window, ms):
+            return dict(
+                dst=z_grouped[:, :, ms, t].rearrange("p u m -> p m u"),
+                src=window[:].rearrange("p (m u) -> p m u", u=PACK)[:, ms, :],
+            )
+
+        early, last = order[:-1], order[-1]
+        windows = {t: sb([P, H], F32, f"d{t}") for t in early}
+        for t in early:
+            nc.vector.tensor_copy(out=windows[t][:].indirect(la_sb[:]), in_=ordered[:, 0, t, :])
+        for t in early:
+            nc.vector.tensor_copy(out=windows[t][:].indirect(lb_sb[:]), in_=ordered[:, 1, t, :])
+            part = plane(t, windows[t], slice(0, P))
+            nc.scalar.activation(out=part["dst"], in_=part["src"], func=COPY, scale=gt_cols[t])
+        window = sb([P, H], F32, f"d{last}", tag=f"d{early[0]}")
+        nc.vector.tensor_copy(out=window[:].indirect(la_sb[:]), in_=ordered[:, 0, last, :])
+        z2_codes = sb([P, N], U32, "z2_codes", tag="small")
+        z2_scales = sb([P, N], U8, "z2_scales")
+        quantize(z2_codes[:], z2_scales[:], z2_grouped[:].rearrange("p c j -> p (c j)"))
+        for w in range(3):
+            warm = psum.tile([P, N], F32, name=f"warm{w}", tag=f"bank{PACK + w}")
+            product(warm[:], z2_codes[:, :P], z2_scales[:, :P], z2_codes[:], z2_scales[:])
+        nc.vector.tensor_copy(out=window[:].indirect(lb_sb[:]), in_=ordered[:, 1, last, :])
+        part = plane(last, window, slice(0, VECTOR_SHARE))
+        nc.vector.tensor_scalar(out=part["dst"], in0=part["src"], scalar1=gt_cols[last], scalar2=None, op0=ALU.mult)
+        part = plane(last, window, slice(VECTOR_SHARE, P))
+        nc.scalar.activation(out=part["dst"], in_=part["src"], func=COPY, scale=gt_cols[last])
 
         z_codes = sb([P, H], U32, "z_codes")
         z_scales = sb([P, H], U8, "z_scales")
@@ -191,13 +206,18 @@ def tile_picked_momord_none_po_kernel(
                 rows = slice(u * P, (u + 1) * P)
                 product(bank[:, u, :], z_codes[:, rows], z_scales[:, rows], z2_codes[:, cols], z2_scales[:, cols])
             y = sb([P, PACK, QUARTER], F32, f"y{c}")
+            y_grouped = sb([P, QUARTER, PACK], BF16, f"y_grouped{c}")
+            if c == N // QUARTER - 1:
+                nc.vector.tensor_scalar(
+                    out=y_grouped[:], in0=bank[:].rearrange("p u n -> p n u"), scalar1=OUT_SCALE, scalar2=None, op0=ALU.mult
+                )
             nc.scalar.activation(out=y[:], in_=bank[:], func=COPY, scale=OUT_SCALE)
             nc.sync.dma_start(out_rows[:, :, cols], y[:])
-            y_grouped = sb([P, QUARTER, PACK], BF16, f"y_grouped{c}")
-            nc.vector.tensor_copy(
-                out=y_grouped[:].rearrange("p (c i) u -> p c u i", i=PACK),
-                in_=y[:].rearrange("p u (c i) -> p c u i", i=PACK),
-            )
+            if c < N // QUARTER - 1:
+                nc.vector.tensor_copy(
+                    out=y_grouped[:].rearrange("p (c i) u -> p c u i", i=PACK),
+                    in_=y[:].rearrange("p u (c i) -> p c u i", i=PACK),
+                )
             quantize(y_codes[:, cols], y_scales[:, cols], y_grouped[:].rearrange("p c u -> p (c u)"))
             nc.sync.dma_start(out_words[:, cols], y_codes[:, cols].bitcast(I32))
         for quad in range(4):

@@ -43,8 +43,8 @@ def tile_picked_momord_none_po_kernel(
             nc.sync.dma_start(tile[:], src)
             return tile
 
-        def interleave_rows(dst, src):
-            nc.scalar.copy(
+        def interleave_rows(dst, src, copy=nc.scalar.copy):
+            copy(
                 out=dst.rearrange("p (c i) j -> p c j i", i=PACK),
                 in_=src.rearrange("p j (c i) -> p c j i", i=PACK),
             )
@@ -197,29 +197,32 @@ def tile_picked_momord_none_po_kernel(
             quantize(z_codes[:, rows], z_scales[:, rows], z_grouped[:, u, :, :].rearrange("p m j -> p (m j)"))
         out_rows = out_0.rearrange("(p u) n -> p u n", u=PACK)
         out_words = out_1[0].rearrange("p c r -> p (c r)").bitcast(I32)
+        y = sb([P, PACK, N], F32, "y")
+        for u in range(PACK):
+            rows = slice(u * P, (u + 1) * P)
+            pieces = 2 if u == PACK - 1 else 1
+            width = N // pieces
+            for piece in range(pieces):
+                cols = slice(piece * width, (piece + 1) * width)
+                bank = psum.tile([P, width], F32, name=f"y_bank{u}_{piece}", tag=f"bank{u + PACK * piece}")
+                product(bank[:], z_codes[:, rows], z_scales[:, rows], z2_codes[:, cols], z2_scales[:, cols])
+                if (u + piece) % 2 == 0:
+                    nc.scalar.activation(out=y[:, u, cols], in_=bank[:], func=COPY, scale=OUT_SCALE)
+                else:
+                    nc.vector.tensor_scalar(out=y[:, u, cols], in0=bank[:], scalar1=OUT_SCALE, scalar2=None, op0=ALU.mult)
+            nc.sync.dma_start(out_rows[:, u, :], y[:, u, :])
         y_codes = sb([P, N], U32, "y_codes")
         y_scales = sb([P, N], U8, "y_scales")
-        for c in range(N // QUARTER):
+        y_grouped = [sb([P, QUARTER, PACK], BF16, f"y_grouped{c}") for c in range(4)]
+        for c in range(4):
             cols = slice(c * QUARTER, (c + 1) * QUARTER)
-            bank = psum.tile([P, PACK, QUARTER], F32, name=f"y_bank{c}", tag=f"bank{c}")
-            for u in range(PACK):
-                rows = slice(u * P, (u + 1) * P)
-                product(bank[:, u, :], z_codes[:, rows], z_scales[:, rows], z2_codes[:, cols], z2_scales[:, cols])
-            y = sb([P, PACK, QUARTER], F32, f"y{c}")
-            y_grouped = sb([P, QUARTER, PACK], BF16, f"y_grouped{c}")
-            if c == N // QUARTER - 1:
-                nc.vector.tensor_scalar(
-                    out=y_grouped[:], in0=bank[:].rearrange("p u n -> p n u"), scalar1=OUT_SCALE, scalar2=None, op0=ALU.mult
-                )
-            nc.scalar.activation(out=y[:], in_=bank[:], func=COPY, scale=OUT_SCALE)
-            nc.sync.dma_start(out_rows[:, :, cols], y[:])
-            if c < N // QUARTER - 1:
-                nc.vector.tensor_copy(
-                    out=y_grouped[:].rearrange("p (c i) u -> p c u i", i=PACK),
-                    in_=y[:].rearrange("p u (c i) -> p c u i", i=PACK),
-                )
-            quantize(y_codes[:, cols], y_scales[:, cols], y_grouped[:].rearrange("p c u -> p (c u)"))
-            nc.sync.dma_start(out_words[:, cols], y_codes[:, cols].bitcast(I32))
+            interleave_rows(y_grouped[c][:], y[:, :, cols], nc.vector.tensor_copy if c < 2 else nc.scalar.copy)
+        for c in range(4):
+            cols = slice(c * QUARTER, (c + 1) * QUARTER)
+            quantize(y_codes[:, cols], y_scales[:, cols], y_grouped[c][:].rearrange("p c u -> p (c u)"))
+            if c % 2:
+                cols = slice((c - 1) * QUARTER, (c + 1) * QUARTER)
+                nc.sync.dma_start(out_words[:, cols], y_codes[:, cols].bitcast(I32))
         for quad in range(4):
             queue = nc.scalar if quad % 2 else nc.sync
             queue.dma_start(

@@ -23,7 +23,7 @@ QUARTER = N // 4
 GATE_PITCH = 8
 OUT_SCALE = 0.0625
 ORDER = (2, 0, 1, 3)
-VECTOR_SHARE = 84
+VECTOR_COLS = 320
 
 
 def tile_picked_momord_none_po_kernel(
@@ -181,14 +181,13 @@ def tile_picked_momord_none_po_kernel(
         z2_codes = sb([P, N], U32, "z2_codes", tag="small")
         z2_scales = sb([P, N], U8, "z2_scales")
         quantize(z2_codes[:], z2_scales[:], z2_grouped[:].rearrange("p c j -> p (c j)"))
-        for w in range(3):
-            warm = psum.tile([P, N], F32, name=f"warm{w}", tag=f"bank{PACK + w}")
-            product(warm[:], z2_codes[:, :P], z2_scales[:, :P], z2_codes[:], z2_scales[:])
         nc.vector.tensor_copy(out=window[:].indirect(lb_sb[:]), in_=ordered[:, 1, last, :])
-        part = plane(last, window, slice(0, VECTOR_SHARE))
-        nc.vector.tensor_scalar(out=part["dst"], in0=part["src"], scalar1=gt_cols[last], scalar2=None, op0=ALU.mult)
-        part = plane(last, window, slice(VECTOR_SHARE, P))
-        nc.scalar.activation(out=part["dst"], in_=part["src"], func=COPY, scale=gt_cols[last])
+        by_slot = window[:].rearrange("p (m u) -> p u m", u=PACK)
+        for u in range(PACK):
+            if u % 2 == 0:
+                nc.vector.tensor_scalar(out=z_grouped[:, u, :, last], in0=by_slot[:, u, :], scalar1=gt_cols[last], scalar2=None, op0=ALU.mult)
+            else:
+                nc.scalar.activation(out=z_grouped[:, u, :, last], in_=by_slot[:, u, :], func=COPY, scale=gt_cols[last])
 
         z_codes = sb([P, H], U32, "z_codes")
         z_scales = sb([P, H], U8, "z_scales")
@@ -214,9 +213,13 @@ def tile_picked_momord_none_po_kernel(
         y_codes = sb([P, N], U32, "y_codes")
         y_scales = sb([P, N], U8, "y_scales")
         y_grouped = [sb([P, QUARTER, PACK], BF16, f"y_grouped{c}") for c in range(4)]
-        for c in range(4):
-            cols = slice(c * QUARTER, (c + 1) * QUARTER)
-            interleave_rows(y_grouped[c][:], y[:, :, cols], nc.vector.tensor_copy if c < 2 else nc.scalar.copy)
+        for start in range(0, N, QUARTER):
+            for lo, hi, copy in (
+                (start, min(start + QUARTER, VECTOR_COLS), nc.vector.tensor_copy),
+                (max(start, VECTOR_COLS), start + QUARTER, nc.scalar.copy),
+            ):
+                if lo < hi:
+                    interleave_rows(y_grouped[start // QUARTER][:, lo - start : hi - start, :], y[:, :, lo:hi], copy)
         for c in range(4):
             cols = slice(c * QUARTER, (c + 1) * QUARTER)
             quantize(y_codes[:, cols], y_scales[:, cols], y_grouped[c][:].rearrange("p c u -> p (c u)"))

@@ -162,20 +162,23 @@ def tile_picked_momord_none_po_kernel(
 
         z_grouped = sb([P, PACK, P, PACK], BF16, "z_grouped", tag="planes")
 
-        def plane(t, window, ms):
-            return dict(
-                dst=z_grouped[:, :, ms, t].rearrange("p u m -> p m u"),
-                src=window[:].rearrange("p (m u) -> p m u", u=PACK)[:, ms, :],
-            )
-
         early, last = order[:-1], order[-1]
         windows = {t: sb([P, H], F32, f"d{t}") for t in early}
-        for t in early:
+
+        def put_larger(t):
             nc.vector.tensor_copy(out=windows[t][:].indirect(la_sb[:]), in_=ordered[:, 0, t, :])
-        for t in early:
+
+        put_larger(early[0])
+        for n, t in enumerate(early):
+            if n + 1 < len(early):
+                put_larger(early[n + 1])
             nc.vector.tensor_copy(out=windows[t][:].indirect(lb_sb[:]), in_=ordered[:, 1, t, :])
-            part = plane(t, windows[t], slice(0, P))
-            nc.scalar.activation(out=part["dst"], in_=part["src"], func=COPY, scale=gt_cols[t])
+            nc.scalar.activation(
+                out=z_grouped[:, :, :, t],
+                in_=windows[t][:].rearrange("p (m u) -> p u m", u=PACK),
+                func=COPY,
+                scale=gt_cols[t],
+            )
         window = sb([P, H], F32, f"d{last}", tag=f"d{early[0]}")
         nc.vector.tensor_copy(out=window[:].indirect(la_sb[:]), in_=ordered[:, 0, last, :])
         z2_codes = sb([P, N], U32, "z2_codes", tag="small")

from contextlib import ExitStack

import concourse.mybir as mybir

K, T, S, V, N, H = 512, 2048, 512, 256, 512, 512
FLOPS = 2 * K * S * H + 2 * K * S * N + 2 * S * H * N

F32 = mybir.dt.float32
BF16 = mybir.dt.bfloat16
I32 = mybir.dt.int32
U32 = mybir.dt.uint32
U16 = mybir.dt.uint16
U8 = mybir.dt.uint8
FP8X4 = mybir.dt.float8_e4m3fn_x4
ALU = mybir.AluOpType
COPY = mybir.ActivationFunctionType.Copy

P = 128
PACK = 4
RUN = 8
HALF = H // 2
QUARTER = N // 4
GATE_PITCH = 8
OUT_SCALE = 0.0625
ORDER = (2, 0, 1, 3)
VECTOR_COLS = 320


def tile_picked_momord_none_po_kernel(
    tc, x_words, x_scales, wa, wb, gt, gi, offs, two, la, lb, out_0, out_1, out_2
):
    nc = tc.nc
    with ExitStack() as ctx:
        lists = ctx.enter_context(tc.tile_pool(name="lists", bufs=1))
        keep = ctx.enter_context(tc.tile_pool(name="keep", bufs=1))
        psum = ctx.enter_context(tc.psum_pool(name="psum", bufs=1))

        def sb(shape, dtype, name, tag=None):
            return keep.tile(shape, dtype, name=name, tag=tag or name, align_bytes=64)

        def load_list(src, name):
            tile = lists.tile(list(src.shape), U16, name=name)
            nc.sync.dma_start(tile[:], src)
            return tile

        def interleave_rows(dst, src, copy=nc.scalar.copy):
            copy(
                out=dst.rearrange("p (c i) j -> p c j i", i=PACK),
                in_=src.rearrange("p j (c i) -> p c j i", i=PACK),
            )

        def quantize(codes, scales, grouped):
            nc.vector.quantize_mx(out=codes.bitcast(FP8X4), scales=scales, in_=grouped)

        def product(out, left_codes, left_scales, right_codes, right_scales):
            nc.tensor.matmul_mx(
                out=out,
                lhsT=left_codes.bitcast(FP8X4),
                lhsT_scale=left_scales,
                rhs=right_codes.bitcast(FP8X4),
                rhs_scale=right_scales,
                start=True,
                stop=True,
            )

        table_scales = sb([P, T], U8, "table_scales")
        nc.vector.memset(table_scales[:].bitcast(I32), 0)
        offs_sb = load_list(offs, "offs_sb")
        two_sb = load_list(two, "two_sb")
        wa_rows = wa.rearrange("(p j) c -> p j c", j=PACK)
        wa_raw = [sb([P, PACK, HALF], F32, f"wa_raw{half}") for half in range(2)]
        nc.sync.dma_start(wa_raw[0][:], wa_rows[:, :, :HALF])
        for quad in range(4):
            nc.sync.dma_start(
                table_scales[32 * quad : 32 * quad + 4, :].bitcast(I32),
                x_scales[0, 4 * quad : 4 * quad + 4, :].bitcast(I32),
            )
        nc.sync.dma_start(wa_raw[1][:], wa_rows[:, :, HALF:])
        table_words = sb([P, T], U32, "table_words")
        nc.sync.dma_start(
            table_words[:].bitcast(I32), x_words[0].rearrange("p c r -> p (c r)").bitcast(I32)
        )
        la_sb = load_list(la, "la_sb")
        lb_sb = load_list(lb, "lb_sb")
        wb_raw = sb([P, PACK, N], F32, "wb_raw")
        nc.sync.dma_start(wb_raw[:], wb.rearrange("(p j) c -> p j c", j=PACK))

        def gather_words(offsets, name, tag=None):
            words = sb([P, S], U32, name, tag)
            nc.vector.tensor_copy(
                out=words[:].rearrange("p (t q e) -> p q t e", t=PACK, e=RUN),
                in_=table_words[:].indirect(offsets[:]),
            )
            return words

        def gather_scales(offsets, name, tag=None):
            listed = sb([P, S], U8, name + "_listed", tag)
            nc.vector.tensor_copy(out=listed[:], in_=table_scales[:].indirect(offsets[:]))
            dealt = sb([P, S], U8, name)
            nc.vector.tensor_copy(
                out=dealt[:].bitcast(I32).rearrange("p (t q e) -> p t q e", t=PACK, e=RUN // 4),
                in_=listed[:].bitcast(I32).rearrange("p (q t e) -> p t q e", t=PACK, e=RUN // 4),
            )
            return dealt

        order = ORDER
        xa_scales = gather_scales(offs_sb, "xa_scales", tag="small")
        xb_scales = gather_scales(two_sb, "xb_scales")
        wa_codes = sb([P, H], U32, "wa_codes")
        wa_scales = sb([P, H], U8, "wa_scales")
        for half in range(2):
            cols = slice(half * HALF, (half + 1) * HALF)
            grouped = sb([P, HALF, PACK], BF16, f"wa_grouped{half}", tag=f"grouped{half}")
            interleave_rows(grouped[:], wa_raw[half][:])
            quantize(wa_codes[:, cols], wa_scales[:, cols], grouped[:].rearrange("p c j -> p (c j)"))
        xa_words = gather_words(offs_sb, "xa_words")
        xb_words = gather_words(two_sb, "xb_words")
        a_sb = {}
        for t in order:
            tok = slice(t * P, (t + 1) * P)
            a_sb[t] = sb([P, H], F32, f"a_sb{t}")
            pieces = 2 if t == order[0] else 1
            width = H // pieces
            for piece in range(pieces):
                cols = slice(piece * width, (piece + 1) * width)
                a_bank = psum.tile([P, width], F32, name=f"a_bank{t}_{piece}", tag=f"bank{PACK * piece + t}")
                product(a_bank[:], xa_words[:, tok], xa_scales[:, tok], wa_codes[:, cols], wa_scales[:, cols])
                nc.scalar.copy(out=a_sb[t][:, cols], in_=a_bank[:])

        gates = sb([P, 2 * PACK - 1, GATE_PITCH], F32, "gates", tag="grouped0")
        first_gate = sb([P, 1], F32, "first_gate", tag="small")
        columns = [gates[:, c, 0:1] for c in range(2 * PACK - 1)]
        gi_cols = columns[:PACK]
        gt_cols = dict(zip(order, [first_gate[:]] + columns[PACK:]))
        with nc.allow_non_contiguous_dma(reason="one weight for each partition"):
            for src, cols in ((gi, gi_cols), (gt, gt_cols)):
                by_tile = src.rearrange("(q t e) o -> t q e o", t=PACK, e=RUN)
                for t in range(PACK):
                    nc.sync.dma_start(cols[t], by_tile[t])

        wb_grouped = sb([P, N, PACK], BF16, "wb_grouped", tag="xa_words")
        interleave_rows(wb_grouped[:], wb_raw[:])
        wb_codes = sb([P, N], U32, "wb_codes")
        wb_scales = sb([P, N], U8, "wb_scales")
        quantize(wb_codes[:], wb_scales[:], wb_grouped[:].rearrange("p c j -> p (c j)"))
        z2_rows = sb([P, PACK, N], BF16, "z2_rows", tag="planes")
        for t in range(PACK):
            tok = slice(t * P, (t + 1) * P)
            b_bank = psum.tile([P, N], F32, name=f"b_bank{t}", tag=f"bank{PACK + t}")
            product(b_bank[:], xb_words[:, tok], xb_scales[:, tok], wb_codes[:], wb_scales[:])
            nc.scalar.activation(out=z2_rows[:, t, :], in_=b_bank[:], func=COPY, scale=gi_cols[t])
        z2_grouped = sb([P, N, PACK], BF16, "z2_grouped")
        interleave_rows(z2_grouped[:], z2_rows[:])

        picked = sb([P, 2, PACK, V], F32, "picked")
        for t in order:
            nc.vector.tensor_copy(out=picked[:, 0, t, :], in_=a_sb[t][:].indirect(la_sb[:]))
            nc.vector.tensor_copy(out=picked[:, 1, t, :], in_=a_sb[t][:].indirect(lb_sb[:]))
        ordered = sb([P, 2, PACK, V], F32, "ordered", tag="wb_raw")
        nc.vector.tensor_tensor(out=ordered[:, 0], in0=picked[:, 0], in1=picked[:, 1], op=ALU.max)
        nc.vector.tensor_tensor(out=ordered[:, 1], in0=picked[:, 0], in1=picked[:, 1], op=ALU.min)

        z_grouped = sb([P, PACK, P, PACK], BF16, "z_grouped", tag="planes")

        early, last = order[:-1], order[-1]
        windows = {t: sb([P, H], F32, f"d{t}") for t in early}

        def put_larger(t):
            nc.vector.tensor_copy(out=windows[t][:].indirect(la_sb[:]), in_=ordered[:, 0, t, :])

        put_larger(early[0])
        for n, t in enumerate(early):
            if n + 1 < len(early):
                put_larger(early[n + 1])
            nc.vector.tensor_copy(out=windows[t][:].indirect(lb_sb[:]), in_=ordered[:, 1, t, :])
            nc.scalar.activation(
                out=z_grouped[:, :, :, t],
                in_=windows[t][:].rearrange("p (m u) -> p u m", u=PACK),
                func=COPY,
                scale=gt_cols[t],
            )
        window = sb([P, H], F32, f"d{last}", tag=f"d{early[0]}")
        nc.vector.tensor_copy(out=window[:].indirect(la_sb[:]), in_=ordered[:, 0, last, :])
        z2_codes = sb([P, N], U32, "z2_codes", tag="small")
        z2_scales = sb([P, N], U8, "z2_scales")
        quantize(z2_codes[:], z2_scales[:], z2_grouped[:].rearrange("p c j -> p (c j)"))
        nc.vector.tensor_copy(out=window[:].indirect(lb_sb[:]), in_=ordered[:, 1, last, :])
        by_slot = window[:].rearrange("p (m u) -> p u m", u=PACK)
        for u in range(PACK):
            if u % 2 == 0:
                nc.vector.tensor_scalar(out=z_grouped[:, u, :, last], in0=by_slot[:, u, :], scalar1=gt_cols[last], scalar2=None, op0=ALU.mult)
            else:
                nc.scalar.activation(out=z_grouped[:, u, :, last], in_=by_slot[:, u, :], func=COPY, scale=gt_cols[last])

        z_codes = sb([P, H], U32, "z_codes")
        z_scales = sb([P, H], U8, "z_scales")
        for u in range(PACK):
            rows = slice(u * P, (u + 1) * P)
            quantize(z_codes[:, rows], z_scales[:, rows], z_grouped[:, u, :, :].rearrange("p m j -> p (m j)"))
        out_rows = out_0.rearrange("(p u) n -> p u n", u=PACK)
        out_words = out_1[0].rearrange("p c r -> p (c r)").bitcast(I32)
        y = sb([P, PACK, N], F32, "y")
        for u in range(PACK):
            rows = slice(u * P, (u + 1) * P)
            pieces = 2 if u == PACK - 1 else 1
            width = N // pieces
            for piece in range(pieces):
                cols = slice(piece * width, (piece + 1) * width)
                bank = psum.tile([P, width], F32, name=f"y_bank{u}_{piece}", tag=f"bank{u + PACK * piece}")
                product(bank[:], z_codes[:, rows], z_scales[:, rows], z2_codes[:, cols], z2_scales[:, cols])
                if (u + piece) % 2 == 0:
                    nc.scalar.activation(out=y[:, u, cols], in_=bank[:], func=COPY, scale=OUT_SCALE)
                else:
                    nc.vector.tensor_scalar(out=y[:, u, cols], in0=bank[:], scalar1=OUT_SCALE, scalar2=None, op0=ALU.mult)
            nc.sync.dma_start(out_rows[:, u, :], y[:, u, :])
        y_codes = sb([P, N], U32, "y_codes")
        y_scales = sb([P, N], U8, "y_scales")
        y_grouped = [sb([P, QUARTER, PACK], BF16, f"y_grouped{c}") for c in range(4)]
        for start in range(0, N, QUARTER):
            for lo, hi, copy in (
                (start, min(start + QUARTER, VECTOR_COLS), nc.vector.tensor_copy),
                (max(start, VECTOR_COLS), start + QUARTER, nc.scalar.copy),
            ):
                if lo < hi:
                    interleave_rows(y_grouped[start // QUARTER][:, lo - start : hi - start, :], y[:, :, lo:hi], copy)
        for c in range(4):
            cols = slice(c * QUARTER, (c + 1) * QUARTER)
            quantize(y_codes[:, cols], y_scales[:, cols], y_grouped[c][:].rearrange("p c u -> p (c u)"))
            if c % 2:
                cols = slice((c - 1) * QUARTER, (c + 1) * QUARTER)
                nc.sync.dma_start(out_words[:, cols], y_codes[:, cols].bitcast(I32))
        for quad in range(4):
            queue = nc.scalar if quad % 2 else nc.sync
            queue.dma_start(
                out_2[0, 4 * quad : 4 * quad + 4, :].bitcast(I32),
                y_scales[32 * quad : 32 * quad + 4, :].bitcast(I32),
            )
